import numpy as np
import ml_dtypes


def mxq(x, axis, fmt="e4m3"):
    dtype, down = {"e4m3": (ml_dtypes.float8_e4m3fn, 7), "e5m2": (ml_dtypes.float8_e5m2, 14)}[fmt]
    v = np.moveaxis(np.asarray(x, np.float32).astype(ml_dtypes.bfloat16).astype(np.float64), axis, -1)
    blocks = v.reshape(v.shape[:-1] + (-1, 32))
    amax = np.abs(blocks).max(-1, keepdims=True)
    byte = np.maximum(np.where(amax > 0, np.frexp(amax)[1] - 1 + 127, 0) - down, 1)
    scale = np.exp2(byte - 127.0)
    codes = (blocks / scale).astype(np.float32).astype(dtype).astype(np.float64)
    return np.moveaxis((codes * scale).reshape(v.shape), -1, axis)


WIDE = False


def mx_kscale(k):
    if not WIDE:
        return np.ones(k)
    levels = np.array([10, -10, 5, -5, 0])
    if k % 512:
        return np.exp2(np.random.permutation(np.resize(levels, k // 32))).repeat(32)
    a = np.empty((k // 512, 16))
    for p in range(k // 512):
        a[p, :8] = np.random.permutation(np.resize(levels, 8))
        for g in range(8):
            far = levels[np.abs(levels - a[p, g]) >= 10]
            a[p, g + 8] = far[np.random.randint(len(far))]
    return np.exp2(a.ravel()).repeat(32)


BF16 = ml_dtypes.bfloat16


def bf(x):
    return np.asarray(x, np.float32).astype(BF16)


def f64(x):
    return np.asarray(x).astype(np.float64)


T, S, Z, A = 2048, 2048, 512, 1024


def setup_inputs():
    s = mx_kscale(S)
    t = mx_kscale(T)
    slopes = np.random.standard_normal((T, S)) * s
    recon = np.random.standard_normal((S, Z)) / np.sqrt(S) / s[:, None]
    gain = 1 + 0.1 * np.random.standard_normal(Z)
    frame_weight = (1 + 0.1 * np.random.standard_normal(T)) * t
    commands = np.random.standard_normal((T, A)) / np.sqrt(T) / t[:, None]
    return {"slopes": bf(slopes),
            "recon": bf(recon),
            "gain": bf(gain),
            "frame_weight": bf(frame_weight),
            "commands": bf(commands)}


def reference(slopes, recon, gain, frame_weight, commands):
    modes = mxq(f64(slopes), 1, "e4m3") @ mxq(f64(recon), 0, "e4m3")
    h = np.tanh(modes * f64(gain)[None, :]) * f64(frame_weight)[:, None]
    return mxq(h, 0, "e4m3").T @ mxq(f64(commands), 0, "e4m3")

from contextlib import ExitStack

import concourse.mybir as mybir
from concourse.masks import make_identity

T, S, Z, A = 2048, 2048, 512, 1024
FLOPS = 2 * T * S * Z + 2 * T * Z * A

F32 = mybir.dt.float32
BF16 = mybir.dt.bfloat16
U32 = mybir.dt.uint32
U8 = mybir.dt.uint8
FP8X4 = mybir.dt.float8_e4m3fn_x4
MULT = mybir.AluOpType.mult
TANH = mybir.ActivationFunctionType.Tanh

P = 128
PACK = 4
K_PASS = P * PACK
BANK = 512
PASSES = 4
TILES = T // P
RAW_BUFS = 10
XG_BUFS = 4
XC_BUFS = 6
GROUPED_BUFS = 8
ORDER = [
    ("lg",), ("lxh", 0, 0), ("lrh", 0, 0), ("lxh", 0, 1), ("lrh", 0, 1), ("tg",), ("eg",), ("lx", 1),
    ("lr", 1), ("lx", 2), ("lr", 2), ("lx", 3), ("lr", 3), ("IR", "V", 0, 0), ("IR", "S", 0, 1), ("IR", "V", 0, 2),
    ("IR", "V", 0, 3), ("T", 0, 0), ("T", 0, 1), ("E", "S", 0, 0), ("E", "S", 0, 1), ("QR", 0), ("Q", 0), ("IR", "V", 1, 0),
    ("IR", "V", 1, 1), ("IR", "V", 1, 2), ("IR", "S", 1, 3), ("T", 1, 0), ("T", 1, 1), ("lc", 0), ("E", "S", 1, 0), ("E", "S", 1, 1),
    ("M", 0, 0), ("QR", 1), ("Q", 1), ("IR", "S", 2, 0), ("IR", "V", 2, 1), ("IR", "V", 2, 2), ("IR", "V", 2, 3), ("T", 2, 0),
    ("T", 2, 1), ("E", "S", 2, 0), ("E", "S", 2, 1), ("M", 0, 1), ("M", 1, 0), ("M", 1, 1), ("QR", 2), ("lc", 1),
    ("lx", 4), ("Q", 2), ("lx", 5), ("IR", "V", 3, 0), ("IR", "S", 3, 1), ("IR", "S", 3, 2), ("IR", "S", 3, 3), ("T", 3, 0),
    ("T", 3, 1), ("IC", "V", 0, 0), ("IC", "V", 0, 1), ("E", "S", 3, 0), ("E", "S", 3, 1), ("M", 0, 2), ("M", 2, 0), ("M", 1, 2),
    ("M", 2, 1), ("M", 2, 2), ("QR", 3), ("Q", 3), ("lc", 2), ("IC", "V", 1, 0), ("IC", "S", 1, 1), ("QC", 0),
    ("T", 4, 0), ("T", 4, 1), ("lx", 6), ("T", 5, 0), ("T", 5, 1), ("M", 0, 3), ("M", 3, 0), ("M", 1, 3),
    ("M", 3, 1), ("M", 2, 3), ("M", 3, 2), ("M", 3, 3), ("lx", 7), ("E", "S", 4, 0), ("E", "S", 4, 1), ("E", "S", 5, 0),
    ("E", "S", 5, 1), ("IC", "S", 2, 0), ("QC", 1), ("IC", "S", 2, 1), ("lc", 4), ("Q", 4), ("lw",), ("G", 0),
    ("G", 1), ("G", 2), ("G", 3), ("Q", 5), ("QC", 2), ("T", 6, 0), ("T", 6, 1), ("lx", 8),
    ("IC", "V", 4, 0), ("T", 7, 0), ("T", 7, 1), ("IC", "V", 4, 1), ("lx", 9), ("lc", 5), ("E", "S", 6, 0), ("E", "S", 6, 1),
    ("M", 4, 0), ("E", "S", 7, 0), ("M", 4, 1), ("M", 4, 2), ("M", 4, 3), ("E", "S", 7, 1), ("M", 5, 0), ("M", 5, 1),
    ("M", 5, 2), ("M", 5, 3), ("Q", 6), ("A", 0), ("QC", 4), ("A", 1), ("A", 2), ("A", 3),
    ("G", 4), ("Q", 7), ("lc", 3), ("T", 8, 0), ("T", 8, 1), ("lx", 10), ("G", 5), ("T", 9, 0),
    ("T", 9, 1), ("lx", 11), ("E", "S", 8, 0), ("E", "S", 8, 1), ("M", 6, 0), ("E", "S", 9, 0), ("M", 6, 1), ("M", 6, 2),
    ("M", 6, 3), ("E", "S", 9, 1), ("M", 7, 0), ("M", 7, 1), ("M", 7, 2), ("M", 7, 3), ("W", 0, 256, 512), ("W", 0, 0, 256),
    ("Q", 8), ("lc", 6), ("A", 4), ("IC", "S", 5, 0), ("G", 6), ("Q", 9), ("IC", "V", 5, 1), ("T", 10, 0),
    ("T", 10, 1), ("lx", 12), ("A", 5), ("G", 7), ("QH", 0, 0, 512), ("T", 11, 0), ("T", 11, 1), ("lx", 13),
    ("E", "S", 10, 0), ("E", "S", 10, 1), ("E", "S", 11, 0), ("M", 8, 0), ("M", 8, 1), ("M", 8, 2), ("M", 8, 3), ("E", "S", 11, 1),
    ("M", 9, 0), ("M", 9, 1), ("M", 9, 2), ("M", 9, 3), ("lc", 7), ("QC", 5), ("Q", 10), ("A", 6),
    ("IC", "V", 3, 0), ("G", 8), ("Q", 11), ("IC", "S", 3, 1), ("T", 12, 0), ("T", 12, 1), ("lx", 14), ("A", 7),
    ("G", 9), ("T", 13, 0), ("T", 13, 1), ("lx", 15), ("E", "S", 12, 0), ("E", "S", 12, 1), ("E", "S", 13, 0), ("M", 10, 0),
    ("M", 10, 1), ("M", 10, 2), ("M", 10, 3), ("E", "S", 13, 1), ("M", 11, 0), ("M", 11, 1), ("M", 11, 2), ("M", 11, 3),
    ("QC", 3), ("Q", 12), ("W", 1, 256, 512), ("W", 1, 0, 256), ("A", 8), ("G", 10), ("Q", 13), ("IC", "S", 6, 0),
    ("T", 14, 0), ("T", 14, 1), ("IC", "S", 6, 1), ("A", 9), ("G", 11), ("T", 15, 0), ("T", 15, 1), ("E", "S", 14, 0),
    ("E", "S", 14, 1), ("E", "S", 15, 0), ("M", 12, 0), ("M", 12, 1), ("M", 12, 2), ("M", 12, 3), ("E", "S", 15, 1), ("QH", 1, 0, 512),
    ("M", 13, 0), ("M", 13, 1), ("M", 13, 2), ("M", 13, 3), ("QC", 6), ("Q", 14), ("A", 10), ("G", 12),
    ("Q", 15), ("A", 11), ("G", 13), ("M", 14, 0), ("M", 14, 1), ("M", 14, 2), ("M", 14, 3), ("M", 15, 0),
    ("M", 15, 1), ("M", 15, 2), ("M", 15, 3), ("R", 0, 0, 0), ("R", 0, 1, 0), ("R", 0, 2, 0), ("R", 0, 3, 0), ("IC", "S", 7, 0),
    ("IC", "S", 7, 1), ("W", 2, 256, 512), ("W", 2, 0, 256), ("A", 12), ("G", 14), ("A", 13), ("G", 15), ("QC", 7),
    ("QH", 2, 0, 512), ("R", 1, 0, 0), ("R", 1, 1, 0), ("R", 1, 2, 0), ("R", 1, 3, 0), ("A", 14), ("A", 15), ("R", 1, 0, 1),
    ("R", 1, 1, 1), ("R", 1, 2, 1), ("R", 1, 3, 1), ("W", 3, 0, 128), ("R", 0, 0, 1), ("R", 0, 1, 1), ("R", 0, 2, 1), ("R", 0, 3, 1),
    ("W", 3, 128, 256), ("QH", 3, 0, 128), ("W", 3, 256, 384), ("QH", 3, 128, 256), ("W", 3, 384, 512), ("QH", 3, 256, 384), ("QH", 3, 384, 512), ("R", 0, 0, 2),
    ("R", 0, 0, 3), ("R", 0, 1, 2), ("R", 0, 1, 3), ("R", 0, 2, 2), ("R", 0, 2, 3), ("R", 0, 3, 2), ("R", 0, 3, 3), ("R", 1, 0, 2),
    ("R", 1, 0, 3), ("R", 1, 1, 2), ("R", 1, 1, 3), ("R", 1, 2, 2), ("R", 1, 2, 3), ("R", 1, 3, 2), ("R", 1, 3, 3), ("O", "S", 0, 0),
    ("st", 0, 0), ("O", "S", 0, 1), ("st", 0, 1), ("O", "S", 0, 2), ("st", 0, 2), ("O", "V", 0, 3), ("st", 0, 3), ("O", "V", 1, 0),
    ("st", 1, 0), ("O", "V", 1, 1), ("st", 1, 1), ("O", "S", 1, 2), ("st", 1, 2), ("O", "S", 1, 3), ("st", 1, 3),
]


def tile_modal_response_estimate_s7_kernel(tc, slopes, recon, gain, frame_weight, commands, out):
    nc = tc.nc
    with ExitStack() as ctx:
        sb = ctx.enter_context(tc.tile_pool(name="sb", bufs=1))
        ps = ctx.enter_context(tc.psum_pool(name="ps", bufs=1))
        ctx.enter_context(tc.manual_schedule())

        def tiles(name, count, shape, dtype):
            return [sb.tile(shape, dtype, name="%s%d" % (name, i), align_bytes=64) for i in range(count)]

        banks = [ps.tile([P, BANK], F32, name="bank%d" % b) for b in range(8)]
        ident = sb.tile([P, P], F32, name="ident")
        warm = sb.tile([P, 8], F32, name="warm")
        gain_rows = sb.tile([P, PACK], BF16, name="gain_rows")
        gain_all = sb.tile([P, Z], BF16, name="gain_all")
        weight = sb.tile([P, PASSES, PACK], BF16, name="weight")
        x_raw = tiles("x_raw", RAW_BUFS, [P, S], BF16)
        x_grouped = tiles("x_grouped", XG_BUFS, [P, S], BF16)
        x_codes = tiles("x_codes", XC_BUFS, [P, PASSES * P], U32)
        x_scales = tiles("x_scales", XC_BUFS, [P, PASSES * P], U8)
        r_raw = [None] + tiles("r_raw", PASSES - 1, [P, PACK, Z], BF16)
        r_first = tiles("r_first", 2, [P, PACK, Z // 2], BF16)
        r_codes = tiles("r_codes", PASSES, [P, Z], U32)
        r_scales = tiles("r_scales", PASSES, [P, Z], U8)
        c_raw = tiles("c_raw", 2 * PASSES, [P, PACK, BANK], BF16)
        c_codes = tiles("c_codes", 2 * PASSES, [P, BANK], U32)
        c_scales = tiles("c_scales", 2 * PASSES, [P, BANK], U8)
        grouped = tiles("grouped", GROUPED_BUFS, [P, BANK * PACK], BF16)
        limited = tiles("limited", 2, [P, PACK, Z], F32)
        h_grouped = tiles("h_grouped", 2, [P, Z * PACK], BF16)
        h_codes = tiles("h_codes", PASSES, [P, Z], U32)
        h_scales = tiles("h_scales", PASSES, [P, Z], U8)
        result = tiles("result", 8, [P, BANK], F32)

        slopes_v = slopes.rearrange("(g m t) s -> g t m s", m=P, t=PACK)
        recon_v = recon.rearrange("(s p j) z -> s p j z", p=P, j=PACK)
        commands_v = commands.rearrange("(g p j) a -> g p j a", p=P, j=PACK)

        def load_x(i):
            nc.sync.dma_start(out=x_raw[i % RAW_BUFS][:], in_=slopes_v[i // PACK, i % PACK])

        def load_r(s):
            nc.sync.dma_start(out=r_raw[s][:], in_=recon_v[s])

        def load_r_half(s, half):
            cols = slice(half * Z // 2, (half + 1) * Z // 2)
            nc.sync.dma_start(out=r_first[half][:], in_=recon_v[s][:, :, cols])

        def load_c(unit):
            half, g = divmod(unit, PASSES)
            cols = slice(half * BANK, (half + 1) * BANK)
            nc.sync.dma_start(out=c_raw[unit][:], in_=commands_v[g][:, :, cols])

        def load_x_half(i, half):
            cols = slice(half * S // 2, (half + 1) * S // 2)
            nc.sync.dma_start(out=x_raw[i % RAW_BUFS][:, cols], in_=slopes_v[i // PACK, i % PACK][:, cols])

        def t_bank(i, half):
            return banks[2 * (i % 2) + half]

        def m_bank(i):
            return banks[4 + i % 4]

        def turn(i, half):
            words = x_raw[i % RAW_BUFS][:].bitcast(F32)
            for s in (2 * half, 2 * half + 1):
                for u in range(2):
                    slot = 2 * (s % 2) + u
                    nc.tensor.transpose(
                        out=t_bank(i, half)[:, slot * P : (slot + 1) * P],
                        in_=words[:, 256 * s + u : 256 * (s + 1) : 2],
                        identity=ident[:],
                    )

        def empty_turned(eng, i, half):
            dst = x_grouped[i % XG_BUFS][:].bitcast(F32)[:, half * BANK : (half + 1) * BANK]
            copies[eng](
                out=dst.rearrange("p (s r u) -> p s r u", s=2, u=2),
                in_=t_bank(i, half)[:].rearrange("p (s u r) -> p s r u", s=2, u=2),
            )

        def quant_x(i):
            nc.vector.quantize_mx(
                out=x_codes[i % XC_BUFS][:].bitcast(FP8X4),
                scales=x_scales[i % XC_BUFS][:],
                in_=x_grouped[i % XG_BUFS][:],
            )

        def interleave(copy, dst, raw, c0, c1, base):
            copy(
                out=dst[:, (c0 - base) * PACK : (c1 - base) * PACK].rearrange("p (c i t) -> p c t i", i=4, t=PACK),
                in_=raw[:, :, c0:c1].rearrange("p t (c i) -> p c t i", i=4),
            )

        def group_r(eng, s, part):
            if s == 0:
                c0 = part % 2 * 128
                interleave(copies[eng], grouped[4], r_first[part // 2], c0, c0 + 128, c0 - part * 128)
            else:
                interleave(copies[eng], grouped[4 + s], r_raw[s], part * 128, (part + 1) * 128, 0)

        def quant_r(s):
            nc.vector.quantize_mx(out=r_codes[s][:].bitcast(FP8X4), scales=r_scales[s][:], in_=grouped[4 + s][:])

        def group_c(eng, unit, part):
            interleave(copies[eng], grouped[unit], c_raw[unit], part * 256, (part + 1) * 256, 0)

        def quant_c(unit):
            nc.vector.quantize_mx(
                out=c_codes[unit][:].bitcast(FP8X4), scales=c_scales[unit][:], in_=grouped[unit % GROUPED_BUFS][:]
            )

        def modes_pass(i, s):
            cols = slice(s * P, (s + 1) * P)
            nc.tensor.matmul_mx(
                out=m_bank(i)[:],
                lhsT=x_codes[i % XC_BUFS][:, cols].bitcast(FP8X4),
                lhsT_scale=x_scales[i % XC_BUFS][:, cols],
                rhs=r_codes[s][:].bitcast(FP8X4),
                rhs_scale=r_scales[s][:],
                start=(s == 0),
                stop=(s == PASSES - 1),
            )

        def modes(i):
            for s in range(PASSES):
                modes_pass(i, s)

        def apply_gain(i):
            g, t = divmod(i, PACK)
            nc.vector.tensor_tensor(out=limited[g % 2][:, t, :], in0=m_bank(i)[:], in1=gain_all[:], op=MULT)

        def limit(i):
            g, t = divmod(i, PACK)
            nc.scalar.activation(out=limited[g % 2][:, t, :], in_=limited[g % 2][:, t, :], func=TANH)

        def weigh(g, z0, z1):
            nc.vector.tensor_tensor(
                out=h_grouped[g % 2][:, z0 * PACK : z1 * PACK].rearrange("p (c i t) -> p c t i", i=2, t=PACK),
                in0=limited[g % 2][:, :, z0:z1].rearrange("p t (c i) -> p c t i", i=2),
                in1=weight[:, g, :].unsqueeze(1).unsqueeze(3).broadcast_to([P, (z1 - z0) // 2, PACK, 2]),
                op=MULT,
            )

        def quant_h(g, z0, z1):
            nc.vector.quantize_mx(
                out=h_codes[g][:, z0:z1].bitcast(FP8X4),
                scales=h_scales[g][:, z0:z1],
                in_=h_grouped[g % 2][:, z0 * PACK : z1 * PACK],
            )

        def response_pass(half, zc, g):
            cols = slice(zc * P, (zc + 1) * P)
            unit = half * PASSES + g
            nc.tensor.matmul_mx(
                out=banks[half * 4 + zc][:],
                lhsT=h_codes[g][:, cols].bitcast(FP8X4),
                lhsT_scale=h_scales[g][:, cols],
                rhs=c_codes[unit][:].bitcast(FP8X4),
                rhs_scale=c_scales[unit][:],
                start=(g == 0),
                stop=(g == PASSES - 1),
            )

        def empty_result(eng, half, zc):
            copies[eng](out=result[half * 4 + zc][:], in_=banks[half * 4 + zc][:])

        def store(half, zc):
            nc.sync.dma_start(out=out[zc * P : (zc + 1) * P, half * BANK : (half + 1) * BANK], in_=result[half * 4 + zc][:])

        def load_gain():
            nc.sync.dma_start(out=gain_rows[:], in_=gain.rearrange("(p c) -> p c", c=PACK))

        def load_weight():
            nc.sync.dma_start(out=weight[:], in_=frame_weight.rearrange("(g p t) -> p g t", p=P, t=PACK))

        def turn_gain():
            gain_words = gain_rows[:].bitcast(F32)
            for u in range(2):
                nc.tensor.transpose(
                    out=banks[7][:, u * P : (u + 1) * P], in_=gain_words[:, u : u + 1].to_broadcast([P, P]), identity=ident[:]
                )

        def empty_gain():
            nc.vector.tensor_copy(
                out=gain_all[:].bitcast(F32).rearrange("p (n u) -> p n u", u=2),
                in_=banks[7][:, 0 : 2 * P].rearrange("p (u n) -> p n u", u=2),
            )

        copies = {"V": nc.vector.tensor_copy, "S": nc.scalar.copy}
        actions = {
            "lx": load_x, "lxh": load_x_half, "lr": load_r, "lrh": load_r_half, "lc": load_c, "lg": load_gain, "lw": load_weight,
            "tg": turn_gain, "eg": empty_gain, "T": turn, "E": empty_turned, "Q": quant_x, "IR": group_r, "QR": quant_r,
            "IC": group_c, "QC": quant_c, "M": modes_pass, "G": apply_gain, "A": limit, "W": weigh, "QH": quant_h,
            "R": response_pass, "O": empty_result, "st": store,
        }
        nc.vector.memset(warm[:], 0.0)
        nc.scalar.activation(out=warm[:, 4:5], in_=warm[:, 0:1], func=TANH)
        make_identity(nc, ident[:])
        for step in ORDER:
            actions[step[0]](*step[1:])
